import numpy as np, ml_dtypes
CORES = [1,17,65,89,97,113]
N = 6
import mx_ref
NC, NB = 128, 3
A = np.float32(0.0125)
SRC = [[(r - i) % N for i in range(NB)] for r in range(N)]
BF = ml_dtypes.bfloat16
def cut(t, i, w=512):
    return t[:, w * i:w * i + w]
def tile(rs):
    return np.stack(rs, axis=2).reshape(128, -1).astype(BF)
def pk(c, s, i=0):
    return (np.ascontiguousarray(c[:, 512 * i:512 * i + 512]), mx_ref.live(s[:, 128 * i:128 * i + 128]))
def raw(rng):
    def f(*shape):
        return mx_ref.flush((rng.standard_normal(shape, dtype=np.float32) * np.exp2(rng.integers(-2, 3, shape[:-1] + (1,)))).astype(BF))
    return {"q": f(N, 128, 4 * NC), "k": f(N, 128, 4 * 512), "v": f(N, 128, 512)}
def raw_blocks(rng):
    d = raw(rng)
    for k in ("v",): d[k] = mx_ref.spread(d[k], rng, 4)
    for k in ("q", "k"): d[k] = mx_ref.spread(d[k], rng, 1)
    return d
def raw_wide(rng):
    d = raw(rng)
    for k in ("v",): d[k] = mx_ref.flush((d[k].astype(np.float32) * np.exp2(rng.integers(-8, 9, (N, 1, 1))).astype(np.float32)).astype(BF))
    return d
def raw_sharp(rng):
    d = raw(rng); v = d["q"].astype(np.float32).reshape(N, 128, -1, 4)
    d["q"] = mx_ref.flush((v * np.exp2(rng.integers(-2, 4, (N, 1, v.shape[2], 1))).astype(np.float32)).reshape(d["q"].shape).astype(BF))
    return d
def raw_offset(rng):
    d = raw(rng); v = d["k"].astype(np.float32).reshape(N, 128, -1, 4)
    d["k"] = mx_ref.flush((v + 12 * rng.standard_normal((1, 128, 1, 4), dtype=np.float32)).reshape(d["k"].shape).astype(BF))
    return d
def pack(d, rng):
    o = {"q": d["q"]}
    for m in ("k", "v"):
        t = d[m]; c = np.zeros(t.shape, np.uint8); s = np.zeros((N, 128, t.shape[2] // 4), np.uint8)
        for r in range(N):
            for i in range(t.shape[2] // 512):
                a, b = mx_ref.quantize(cut(t[r], i)); c[r][:, 512 * i:512 * i + 512] = a; s[r][:, 128 * i:128 * i + 128] = mx_ref.plane(b, rng)
        o[m + "c"], o[m + "s"] = c, s
    return o
def setup_inputs(rng):
    return pack(raw(rng), rng)
def setup_inputs_blocks(rng):
    return pack(raw_blocks(rng), rng)
def setup_inputs_offset(rng):
    return pack(raw_offset(rng), rng)
def setup_inputs_sharp(rng):
    return pack(raw_sharp(rng), rng)
def setup_inputs_wide(rng):
    return pack(raw_wide(rng), rng)
def reference(q, kc, ks, vc, vs, own=None):
    ONE = mx_ref.quantize(np.ones((128, 512), BF))
    K = [[pk(kc[j], ks[j], b) for b in range(4)] for j in range(N)]; V = [pk(vc[j], vs[j]) for j in range(N)]
    lo = np.zeros((N, NB, NC), np.float32); hi = lo.copy(); c = lo.copy(); w = lo.copy(); wlo = lo.copy(); whi = lo.copy(); p = np.zeros((N, NB, 128, 4 * NC), BF); o = np.zeros((N, 128, NC), np.float32)
    for r in range(N):
        Q = mx_ref.quantize(q[r])
        S = [[mx_ref.matmul(K[j][b], Q) * A for b in range(4)] for j in SRC[r]]
        lo[r] = [np.max(s, axis=(0, 1)) for s in S]; hi[r] = lo[r].max(axis=0) + 8
        c[r] = lo[r] if own is None else own["c"][r]
        for i in range(NB):
            p[r][i] = tile([np.exp(np.maximum(s - c[r][i], -20).astype(np.float64)).astype(np.float32) for s in S[i]])
        use = p[r] if own is None else own["p"][r]
        e = np.exp((c[r] - c[r].max(axis=0)).astype(np.float64)); wlo[r] = e * (1 - 4e-5); whi[r] = e * (1 + 4e-5)
        w[r] = e if own is None else own["w"][r]
        num = den = 0
        for i in range(NB):
            P = mx_ref.quantize(use[i])
            num = num + w[r][i].astype(np.float64) * mx_ref.matmul(V[SRC[r][i]], P); den = den + w[r][i].astype(np.float64) * mx_ref.matmul(ONE, P)
        o[r] = (num / den).astype(np.float32)
    return {"c": c, "c__lo": lo, "c__hi": hi, "p": p, "w": w, "w__lo": wlo, "w__hi": whi, "o": o}

@@ -1,0 +1,315 @@
+import math
+from concourse.mybir import dt, AluOpType, AxisListType, ActivationFunctionType
+
+NSIM = 128
+NB = 3
+SCALE = 0.0125
+FLOOR = math.exp(-20.0)
+W = 640
+HALF = ((0, 320), (320, 640))
+KCOL = (0, 128, 384, 512)
+VCOL = 256
+STCOL = (0, 384)
+NEV = 100
+NENG = 8
+
+SCRATCH = {
+    "qt": ("sbuf", [128, 512], "bfloat16"),
+    "qc": ("sbuf", [128, 128], "float8_e4m3fn_x4"),
+    "qs": ("sbuf", [128, 128], "uint8"),
+    "onet": ("sbuf", [128, 512], "bfloat16"),
+    "onec": ("sbuf", [128, 128], "float8_e4m3fn_x4"),
+    "ones": ("sbuf", [128, 128], "uint8"),
+    "rc": ("sbuf", [128, 320], "float8_e4m3fn_x4"),
+    "rs": ("sbuf", [128, 320], "uint8"),
+    "zero": ("sbuf", [128, 128], "float32"),
+    "wone": ("sbuf", [128, 128], "float32"),
+    "red": ("sbuf", [128, 8], "float32"),
+    "mc": ("sbuf", [128, 4], "float32"),
+    "z01": ("sbuf", [128, 128], "float32"),
+    "z2": ("sbuf", [128, 128], "float32"),
+    "c01": ("sbuf", [128, 128], "float32"),
+    "c2": ("sbuf", [128, 128], "float32"),
+    "dc": ("sbuf", [128, 128], "float32"),
+    "al": ("sbuf", [128, 128], "float32"),
+    "tn": ("sbuf", [128, 128], "float32"),
+    "td": ("sbuf", [128, 128], "float32"),
+    "den": ("sbuf", [128, 128], "float32"),
+    "rd": ("sbuf", [128, 128], "float32"),
+    "num": ("sbuf", [128, 128], "float32"),
+    "ot": ("sbuf", [128, 128], "float32"),
+    "pss": ("psum", [128, 2048], "float32"),
+    "pst": ("psum", [128, 1024], "float32"),
+    "psa": ("psum", [128, 512], "float32"),
+    "psl": ("psum", [128, 512], "float32"),
+}
+for _i in range(NB):
+    SCRATCH["bc%d" % _i] = ("sbuf", [128, W], "float8_e4m3fn_x4")
+    SCRATCH["bs%d" % _i] = ("sbuf", [128, W], "uint8")
+    SCRATCH["t%d" % _i] = ("sbuf", [128, 512], "float32")
+    SCRATCH["pt%d" % _i] = ("sbuf", [128, 512], "bfloat16")
+    SCRATCH["pc%d" % _i] = ("sbuf", [128, 128], "float8_e4m3fn_x4")
+    SCRATCH["pp%d" % _i] = ("sbuf", [128, 128], "uint8")
+
+SEMAPHORES = ["la", "lb", "lq", "st", "rin", "sent", "a10", "a11", "a20", "a21"] + ["e%d" % _k for _k in range(NEV)]
+
+
+def _engines(mask, k):
+    out, n = 0, 0
+    for e in range(16):
+        if (mask >> e) & 1 and n < k:
+            out |= 1 << e
+            n += 1
+    return out
+
+
+def _plan(T, topo):
+    cores = [int(c) for c in T.cores]
+    n = len(cores)
+    jobs = {}
+    for j, cj in enumerate(cores):
+        dests = [(cores[(j + i) % n], i) for i in range(1, NB)]
+        mates = [c for c in range(NSIM) if topo.chip(c) == topo.chip(cj) and c != cj and T.rank_of(c) is None]
+        same = [c for c in mates if topo.die(c) == topo.die(cj)]
+        other = [c for c in mates if topo.die(c) != topo.die(cj)]
+        direct = [d for d in dests if topo.may_write(cj, d[0])]
+        barred = [d for d in dests if not topo.may_write(cj, d[0])]
+        feeds = []
+        rb = [c for c in other if all(topo.may_write(c, d[0]) for d in dests)][0]
+        feeds.append((rb, 1))
+        jobs[rb] = ("relay", 1, dests)
+        if barred:
+            ra = [c for c in same if all(topo.may_write(c, d[0]) for d in barred)][0]
+            feeds.append((ra, 0))
+            jobs[ra] = ("relay", 0, barred)
+        jobs[cj] = ("rank", feeds, direct)
+    return jobs
+
+
+def rank_program(g, core, T, topo):
+    job = _plan(T, topo).get(core)
+    if job is None:
+        return
+    u8 = dt.uint8
+    sent = [0]
+
+    def send(dst, oc, os_, ic, is_, sem):
+        rid, pid, _ = topo.addr(dst)
+        m = _engines(topo.mask(core, dst), NENG)
+        g.remote_dma(out_ap=oc.bitcast(u8), in_ap=ic.bitcast(u8), remote_sem=sem, local_sem=T.sem.sent, pid=pid,
+                     routing_id=rid, dma_engine_mask=m)
+        g.remote_dma(out_ap=os_, in_ap=is_, remote_sem=sem, local_sem=T.sem.sent, pid=pid, routing_id=rid,
+                     dma_engine_mask=m)
+        sent[0] += 2 * NENG
+
+    if job[0] == "relay":
+        _, h, dests = job
+        a, b = HALF[h]
+        g.wait_ge(T.sem.rin, 2 * NENG)
+        for d, blk in dests:
+            send(d, T["bc%d" % blk][:, a:b], T["bs%d" % blk][:, a:b], T.rc[:], T.rs[:], T.sem["a%d%d" % (blk, h)])
+        g.wait_ge(T.sem.sent, sent[0])
+        return
+
+    _, feeds, direct = job
+    V, S, P, Y = g.vector, g.scalar, g.tensor, g.sync
+    AF, OP = ActivationFunctionType, AluOpType
+    nev = [0]
+
+    def ev():
+        s = T.sem["e%d" % nev[0]]
+        nev[0] += 1
+        return s
+
+    LA, LB, LQ = T.sem.la, T.sem.lb, T.sem.lq
+    Y.dma_start(T.bc0[:, 384:640].bitcast(u8), T.kc[:, 1024:2048]).then_inc(LB, 16)
+    S.dma_start(T.bs0[:, 384:640], T.ks[:, 256:512]).then_inc(LB, 16)
+    Y.dma_start(T.bc0[:, 256:384].bitcast(u8), T.vc[:]).then_inc(LB, 16)
+    S.dma_start(T.bs0[:, 256:384], T.vs[:]).then_inc(LB, 16)
+    Y.dma_start(T.bc0[:, 0:256].bitcast(u8), T.kc[:, 0:1024]).then_inc(LA, 16)
+    S.dma_start(T.bs0[:, 0:256], T.ks[:, 0:256]).then_inc(LA, 16)
+    S.dma_start(T.qt[:], T.q[:]).then_inc(LQ, 16)
+
+    g.wait_ge(LB, 64)
+    waited_a = False
+    for r, h in feeds:
+        if h == 0 and not waited_a:
+            g.wait_ge(LA, 32)
+            waited_a = True
+        a, b = HALF[h]
+        send(r, T.rc[:], T.rs[:], T.bc0[:, a:b], T.bs0[:, a:b], T.sem.rin)
+    if direct and not waited_a:
+        g.wait_ge(LA, 32)
+    a, b = HALF[0]
+    for d, blk in direct:
+        send(d, T["bc%d" % blk][:, a:b], T["bs%d" % blk][:, a:b], T.bc0[:, a:b], T.bs0[:, a:b],
+             T.sem["a%d0" % blk])
+    g.wait_ge(T.sem.sent, sent[0])
+
+    e_one, e_zero, e_w2, e_oq, e_q = ev(), ev(), ev(), ev(), ev()
+    V.memset(T.onet[:], 1.0).then_inc(e_one, 1)
+    V.memset(T.zero[:], 0.0).then_inc(e_zero, 1)
+    V.memset(T.wone[0:1, :], 1.0).then_inc(e_w2, 1)
+    V.wait_ge(e_one, 1)
+    V.quantize_mx(T.onec[:], T.ones[:], T.onet[:]).then_inc(e_oq, 1)
+    V.wait_ge(LQ, 16)
+    V.quantize_mx(T.qc[:], T.qs[:], T.qt[:]).then_inc(e_q, 1)
+
+    stores = [0]
+
+    def store(out, in_):
+        Y.dma_start(out, in_).then_inc(T.sem.st, 16)
+        stores[0] += 16
+
+    Y.wait_ge(e_w2, 1)
+    store(T.w[2:3, :], T.wone[0:1, :])
+
+    e_st = [[ev(), ev()] for _ in range(NB)]
+    e_s = [[ev() for _ in range(4)] for _ in range(NB)]
+    e_t = [[ev() for _ in range(4)] for _ in range(NB)]
+    e_r = [[ev(), ev()] for _ in range(NB)]
+
+    P.wait_ge(e_q, 1)
+    for i in range(NB):
+        bc, bs = T["bc%d" % i], T["bs%d" % i]
+        for h in range(2):
+            if i == 0:
+                P.wait_ge(LA if h == 0 else LB, 32 if h == 0 else 64)
+            else:
+                P.wait_ge(T.sem["a%d%d" % (i, h)], 2 * NENG)
+                P.wait_ge(e_r[i - 1][h], 1)
+            k = STCOL[h]
+            P.matmul_mx(T.pst[:, 512 * h:512 * h + 256], T.qc[:], T.qs[:], bc[:, k:k + 256], bs[:, k:k + 256],
+                        True, True).then_inc(e_st[i][h], 1)
+            for b in (2 * h, 2 * h + 1):
+                if i > 0:
+                    P.wait_ge(e_t[i - 1][b], 1)
+                k = KCOL[b]
+                P.matmul_mx(T.pss[:, 512 * b:512 * b + 128], bc[:, k:k + 128], bs[:, k:k + 128], T.qc[:], T.qs[:],
+                            True, True).then_inc(e_s[i][b], 1)
+
+    def scale_and_max(i):
+        t = T["t%d" % i]
+        for h in range(2):
+            V.wait_ge(e_st[i][h], 1)
+            V.tensor_reduce(T.red[:, 2 * i + h:2 * i + h + 1], T.pst[:, 512 * h:512 * h + 256], AxisListType.X,
+                            OP.max).then_inc(e_r[i][h], 1)
+            for b in (2 * h, 2 * h + 1):
+                S.wait_ge(e_s[i][b], 1)
+                S.activation(t[:, b:512:4], T.pss[:, 512 * b:512 * b + 128], AF.Identity,
+                             scale=SCALE).then_inc(e_t[i][b], 1)
+
+    def spread(z, c, e_z):
+        e_x, e1, e2 = ev(), ev(), ev()
+        V.wait_ge(e_z, 1)
+        V.transpose(c[:], z[:]).then_inc(e_x, 1)
+        V.wait_ge(e_x, 1)
+        S.wait_ge(e_x, 1)
+        V.tensor_copy(c[0:32, 32:64], c[32:64, 32:64]).then_inc(e1, 1)
+        V.tensor_copy(c[32:64, 0:32], c[0:32, 0:32]).then_inc(e1, 1)
+        S.activation(c[64:96, 96:128], c[96:128, 96:128], AF.Copy).then_inc(e1, 1)
+        S.activation(c[96:128, 64:96], c[64:96, 64:96], AF.Copy).then_inc(e1, 1)
+        V.wait_ge(e1, 4)
+        S.wait_ge(e1, 4)
+        V.tensor_copy(c[0:64, 64:128], c[64:128, 64:128]).then_inc(e2, 1)
+        S.activation(c[64:128, 0:64], c[0:64, 0:64], AF.Copy).then_inc(e2, 1)
+        return e2
+
+    scale_and_max(0)
+    scale_and_max(1)
+    e_m, e_z = ev(), ev()
+    for i in range(2):
+        for h in range(2):
+            V.wait_ge(e_r[i][h], 1)
+    V.tensor_reduce(T.mc[:, 0:1], T.red[:, 0:4], AxisListType.X, OP.max).then_inc(e_m, 1)
+    V.wait_ge(e_m, 1)
+    V.wait_ge(e_zero, 1)
+    V.tensor_scalar(T.z01[:], T.zero[:], T.mc[:, 0:1], SCALE, OP.add, OP.mult).then_inc(e_z, 1)
+    e_c01 = spread(T.z01, T.c01, e_z)
+    Y.wait_ge(e_c01, 2)
+    store(T.c[0:1, :], T.c01[0:1, :])
+    store(T.c[1:2, :], T.c01[0:1, :])
+    V.wait_ge(e_c01, 2)
+    e_sub, e_exp, e_p, e_pq = [ev(), ev()], [ev(), ev()], [ev(), ev()], [ev(), ev()]
+    for i in range(2):
+        t = T["t%d" % i]
+        for b in range(4):
+            V.wait_ge(e_t[i][b], 1)
+            V.tensor_tensor(t[:, b:512:4], t[:, b:512:4], T.c01[:], OP.subtract).then_inc(e_sub[i], 1)
+        S.wait_ge(e_sub[i], 4)
+        S.activation(T["pt%d" % i][:], t[:], AF.Exp).then_inc(e_exp[i], 1)
+    e_l01, e_a01 = ev(), ev()
+    P.wait_ge(e_oq, 1)
+    for i in range(2):
+        pt, pc, pp = T["pt%d" % i], T["pc%d" % i], T["pp%d" % i]
+        V.wait_ge(e_exp[i], 1)
+        V.tensor_scalar(pt[:], pt[:], FLOOR, None, OP.max).then_inc(e_p[i], 1)
+        V.wait_ge(e_p[i], 1)
+        V.quantize_mx(pc[:], pp[:], pt[:]).then_inc(e_pq[i], 1)
+        Y.wait_ge(e_p[i], 1)
+        store(T.p[i], pt[:])
+        P.wait_ge(e_pq[i], 1)
+        ml = P.matmul_mx(T.psl[:, 0:128], T.onec[:], T.ones[:], pc[:], pp[:], i == 0, i == 1)
+        ma = P.matmul_mx(T.psa[:, 0:128], T["bc%d" % i][:, VCOL:VCOL + 128], T["bs%d" % i][:, VCOL:VCOL + 128],
+                         pc[:], pp[:], i == 0, i == 1)
+        if i == 1:
+            ml.then_inc(e_l01, 1)
+            ma.then_inc(e_a01, 1)
+
+    scale_and_max(2)
+    e_m2, e_z2 = ev(), ev()
+    V.wait_ge(e_r[2][0], 1)
+    V.wait_ge(e_r[2][1], 1)
+    V.tensor_scalar(T.mc[:, 1:2], T.red[:, 4:5], T.red[:, 5:6], SCALE, OP.max, OP.mult).then_inc(e_m2, 1)
+    V.wait_ge(e_m2, 1)
+    V.tensor_scalar(T.z2[:], T.z01[:], T.mc[:, 1:2], None, OP.max).then_inc(e_z2, 1)
+    e_c2 = spread(T.z2, T.c2, e_z2)
+    Y.wait_ge(e_c2, 2)
+    store(T.c[2:3, :], T.c2[0:1, :])
+    V.wait_ge(e_c2, 2)
+    e_sb, e_ex = [ev() for _ in range(4)], [ev() for _ in range(4)]
+    e_p2, e_pq2 = ev(), ev()
+    for b in range(4):
+        V.wait_ge(e_t[2][b], 1)
+        V.tensor_tensor(T.t2[:, b:512:4], T.t2[:, b:512:4], T.c2[:], OP.subtract).then_inc(e_sb[b], 1)
+        S.wait_ge(e_sb[b], 1)
+        S.activation(T.pt2[:, b:512:4], T.t2[:, b:512:4], AF.Exp).then_inc(e_ex[b], 1)
+    for b in range(4):
+        V.wait_ge(e_ex[b], 1)
+        V.tensor_scalar(T.pt2[:, b:512:4], T.pt2[:, b:512:4], FLOOR, None, OP.max).then_inc(e_p2, 1)
+    V.wait_ge(e_p2, 4)
+    V.quantize_mx(T.pc2[:], T.pp2[:], T.pt2[:]).then_inc(e_pq2, 1)
+    Y.wait_ge(e_p2, 4)
+    store(T.p[2], T.pt2[:])
+    e_l2, e_a2 = ev(), ev()
+    P.wait_ge(e_pq2, 1)
+    P.matmul_mx(T.pst[:, 0:128], T.onec[:], T.ones[:], T.pc2[:], T.pp2[:], True, True).then_inc(e_l2, 1)
+    P.matmul_mx(T.pst[:, 512:640], T.bc2[:, VCOL:VCOL + 128], T.bs2[:, VCOL:VCOL + 128], T.pc2[:], T.pp2[:],
+                True, True).then_inc(e_a2, 1)
+
+    e_dc, e_al, e_td, e_tn, e_den, e_rd, e_num, e_o = ev(), ev(), ev(), ev(), ev(), ev(), ev(), ev()
+    V.tensor_tensor(T.dc[:], T.c01[:], T.c2[:], OP.subtract).then_inc(e_dc, 1)
+    S.wait_ge(e_dc, 1)
+    S.activation(T.al[:], T.dc[:], AF.Exp).then_inc(e_al, 1)
+    Y.wait_ge(e_al, 1)
+    store(T.w[0:1, :], T.al[0:1, :])
+    store(T.w[1:2, :], T.al[0:1, :])
+    V.wait_ge(e_al, 1)
+    V.wait_ge(e_l01, 1)
+    V.tensor_tensor(T.td[:], T.psl[:, 0:128], T.al[:], OP.mult).then_inc(e_td, 1)
+    V.wait_ge(e_a01, 1)
+    V.tensor_tensor(T.tn[:], T.psa[:, 0:128], T.al[:], OP.mult).then_inc(e_tn, 1)
+    V.wait_ge(e_td, 1)
+    V.wait_ge(e_l2, 1)
+    V.tensor_tensor(T.den[:], T.pst[:, 0:128], T.td[:], OP.add).then_inc(e_den, 1)
+    V.wait_ge(e_den, 1)
+    V.reciprocal(T.rd[:], T.den[:]).then_inc(e_rd, 1)
+    V.wait_ge(e_tn, 1)
+    V.wait_ge(e_a2, 1)
+    V.tensor_tensor(T.num[:], T.pst[:, 512:640], T.tn[:], OP.add).then_inc(e_num, 1)
+    V.wait_ge(e_rd, 1)
+    V.wait_ge(e_num, 1)
+    V.tensor_tensor(T.ot[:], T.num[:], T.rd[:], OP.mult).then_inc(e_o, 1)
+    Y.wait_ge(e_o, 1)
+    store(T.o[:], T.ot[:])
+    Y.wait_ge(T.sem.st, stores[0])

@@ -1,4 +1,5 @@
 import math
+from concourse.bass import DstId, RemoteDMATransfer
 from concourse.mybir import dt, AluOpType, AxisListType, ActivationFunctionType
 
 NSIM = 128
@@ -11,7 +12,6 @@ KCOL = (0, 128, 384, 512)
 VCOL = 256
 STCOL = (0, 384)
 NEV = 100
-NENG = 8
 
 SCRATCH = {
     "qt": ("sbuf", [128, 512], "bfloat16"),
@@ -27,6 +27,7 @@ SCRATCH = {
     "red": ("sbuf", [128, 8], "float32"),
     "mc": ("sbuf", [128, 4], "float32"),
     "z01": ("sbuf", [128, 128], "float32"),
+    "z0r": ("sbuf", [128, 128], "float32"),
     "z2": ("sbuf", [128, 128], "float32"),
     "c01": ("sbuf", [128, 128], "float32"),
     "c2": ("sbuf", [128, 128], "float32"),
@@ -51,67 +52,84 @@ for _i in range(NB):
     SCRATCH["pc%d" % _i] = ("sbuf", [128, 128], "float8_e4m3fn_x4")
     SCRATCH["pp%d" % _i] = ("sbuf", [128, 128], "uint8")
 
-SEMAPHORES = ["la", "lb", "lq", "st", "rin", "sent", "a10", "a11", "a20", "a21"] + ["e%d" % _k for _k in range(NEV)]
+SEMAPHORES = (["la", "lb", "lp", "lq", "st", "rinp", "rinc", "sent", "a10", "a11", "a20", "a21"]
+              + ["e%d" % _k for _k in range(NEV)])
 
 
-def _engines(mask, k):
-    out, n = 0, 0
-    for e in range(16):
-        if (mask >> e) & 1 and n < k:
-            out |= 1 << e
-            n += 1
-    return out
+def _split(mask, k):
+    eng = [e for e in range(16) if (mask >> e) & 1]
+    n = len(eng) // k
+    return [sum(1 << e for e in eng[i * n:(i + 1) * n]) for i in range(k)], n
 
 
 def _plan(T, topo):
     cores = [int(c) for c in T.cores]
     n = len(cores)
-    jobs = {}
+    jobs, groups = {}, []
     for j, cj in enumerate(cores):
         dests = [(cores[(j + i) % n], i) for i in range(1, NB)]
         mates = [c for c in range(NSIM) if topo.chip(c) == topo.chip(cj) and c != cj and T.rank_of(c) is None]
-        same = [c for c in mates if topo.die(c) == topo.die(cj)]
-        other = [c for c in mates if topo.die(c) != topo.die(cj)]
-        direct = [d for d in dests if topo.may_write(cj, d[0])]
-        barred = [d for d in dests if not topo.may_write(cj, d[0])]
-        feeds = []
-        rb = [c for c in other if all(topo.may_write(c, d[0]) for d in dests)][0]
-        feeds.append((rb, 1))
-        jobs[rb] = ("relay", 1, dests)
-        if barred:
-            ra = [c for c in same if all(topo.may_write(c, d[0]) for d in barred)][0]
-            feeds.append((ra, 0))
-            jobs[ra] = ("relay", 0, barred)
-        jobs[cj] = ("rank", feeds, direct)
-    return jobs
+        pools = {0: [c for c in mates if topo.die(c) == topo.die(cj)],
+                 1: [c for c in mates if topo.die(c) != topo.die(cj)]}
+        used = []
+        feeds = {0: [], 1: []}
+        for h in (1, 0):
+            for d in dests:
+                if h == 0 and cj not in used and topo.may_write(cj, d[0]):
+                    r = cj
+                else:
+                    r = [c for c in pools[h] if c not in used and topo.may_write(c, d[0])][0]
+                    feeds[h].append(r)
+                used.append(r)
+                groups.append((r, h, [d]))
+        for h in (0, 1):
+            for r in feeds[h]:
+                jobs[r] = ("relay", cj, len(feeds[h]))
+        jobs[cj] = ("rank", feeds)
+    return jobs, groups
 
 
 def rank_program(g, core, T, topo):
-    job = _plan(T, topo).get(core)
+    jobs, groups = _plan(T, topo)
+    job = jobs.get(core)
     if job is None:
         return
     u8 = dt.uint8
     sent = [0]
+    mine = [gr for gr in groups if gr[0] == core]
 
-    def send(dst, oc, os_, ic, is_, sem):
-        rid, pid, _ = topo.addr(dst)
-        m = _engines(topo.mask(core, dst), NENG)
-        g.remote_dma(out_ap=oc.bitcast(u8), in_ap=ic.bitcast(u8), remote_sem=sem, local_sem=T.sem.sent, pid=pid,
-                     routing_id=rid, dma_engine_mask=m)
-        g.remote_dma(out_ap=os_, in_ap=is_, remote_sem=sem, local_sem=T.sem.sent, pid=pid, routing_id=rid,
-                     dma_engine_mask=m)
-        sent[0] += 2 * NENG
+    def send(targets, src, codes):
+        masks, n = _split(topo.mask(core, targets[0][0]), len(targets))
+        trs = []
+        for (dst, out, sem), m in zip(targets, masks):
+            rid, pid, _ = topo.addr(dst)
+            trs.append(RemoteDMATransfer(dst_ids=[DstId(rid=rid, pnc=pid)], dma_engine_mask=m, remote_sem=sem,
+                                         src=src.bitcast(u8) if codes else src,
+                                         dst=out.bitcast(u8) if codes else out))
+            sent[0] += n
+        g.remote_dma_fused(trs, local_sem=T.sem.sent)
+
+    def planes_out(src):
+        for _, h, dests in mine:
+            a, b = HALF[h]
+            send([(d, T["bs%d" % k][:, a:b], T.sem["a%d%d" % (k, h)]) for d, k in dests], src, False)
+
+    def codes_out(src):
+        for _, h, dests in mine:
+            a, b = HALF[h]
+            for d, k in dests:
+                send([(d, T["bc%d" % k][:, a:b], T.sem["a%d%d" % (k, h)])], src, True)
 
     if job[0] == "relay":
-        _, h, dests = job
-        a, b = HALF[h]
-        g.wait_ge(T.sem.rin, 2 * NENG)
-        for d, blk in dests:
-            send(d, T["bc%d" % blk][:, a:b], T["bs%d" % blk][:, a:b], T.rc[:], T.rs[:], T.sem["a%d%d" % (blk, h)])
+        nfeed = _split(topo.mask(job[1], core), job[2])[1]
+        g.wait_ge(T.sem.rinp, nfeed)
+        planes_out(T.rs[:])
+        g.wait_ge(T.sem.rinc, nfeed)
+        codes_out(T.rc[:])
         g.wait_ge(T.sem.sent, sent[0])
         return
 
-    _, feeds, direct = job
+    feeds = job[1]
     V, S, P, Y = g.vector, g.scalar, g.tensor, g.sync
     AF, OP = ActivationFunctionType, AluOpType
     nev = [0]
@@ -121,29 +139,34 @@ def rank_program(g, core, T, topo):
         nev[0] += 1
         return s
 
-    LA, LB, LQ = T.sem.la, T.sem.lb, T.sem.lq
+    arrive = {}
+    for snd, h, dests in groups:
+        for d, k in dests:
+            if d == core:
+                arrive[(k, h)] = _split(topo.mask(snd, d), len(dests))[1] + _split(topo.mask(snd, d), 1)[1]
+
+    LA, LB, LP, LQ = T.sem.la, T.sem.lb, T.sem.lp, T.sem.lq
+    S.dma_start(T.bs0[:, 384:640], T.ks[:, 256:512]).then_inc(LP, 16)
+    S.dma_start(T.bs0[:, 256:384], T.vs[:]).then_inc(LP, 16)
+    S.dma_start(T.bs0[:, 0:256], T.ks[:, 0:256]).then_inc(LP, 16)
     Y.dma_start(T.bc0[:, 384:640].bitcast(u8), T.kc[:, 1024:2048]).then_inc(LB, 16)
-    S.dma_start(T.bs0[:, 384:640], T.ks[:, 256:512]).then_inc(LB, 16)
     Y.dma_start(T.bc0[:, 256:384].bitcast(u8), T.vc[:]).then_inc(LB, 16)
-    S.dma_start(T.bs0[:, 256:384], T.vs[:]).then_inc(LB, 16)
     Y.dma_start(T.bc0[:, 0:256].bitcast(u8), T.kc[:, 0:1024]).then_inc(LA, 16)
-    S.dma_start(T.bs0[:, 0:256], T.ks[:, 0:256]).then_inc(LA, 16)
     S.dma_start(T.qt[:], T.q[:]).then_inc(LQ, 16)
 
-    g.wait_ge(LB, 64)
-    waited_a = False
-    for r, h in feeds:
-        if h == 0 and not waited_a:
-            g.wait_ge(LA, 32)
-            waited_a = True
-        a, b = HALF[h]
-        send(r, T.rc[:], T.rs[:], T.bc0[:, a:b], T.bs0[:, a:b], T.sem.rin)
-    if direct and not waited_a:
-        g.wait_ge(LA, 32)
-    a, b = HALF[0]
-    for d, blk in direct:
-        send(d, T["bc%d" % blk][:, a:b], T["bs%d" % blk][:, a:b], T.bc0[:, a:b], T.bs0[:, a:b],
-             T.sem["a%d0" % blk])
+    a0, b0 = HALF[0]
+    a1, b1 = HALF[1]
+    g.wait_ge(LP, 48)
+    send([(r, T.rs[:], T.sem.rinp) for r in feeds[1]], T.bs0[:, a1:b1], False)
+    if feeds[0]:
+        send([(r, T.rs[:], T.sem.rinp) for r in feeds[0]], T.bs0[:, a0:b0], False)
+    planes_out(T.bs0[:, a0:b0])
+    g.wait_ge(LB, 32)
+    send([(r, T.rc[:], T.sem.rinc) for r in feeds[1]], T.bc0[:, a1:b1], True)
+    g.wait_ge(LA, 16)
+    if feeds[0]:
+        send([(r, T.rc[:], T.sem.rinc) for r in feeds[0]], T.bc0[:, a0:b0], True)
+    codes_out(T.bc0[:, a0:b0])
     g.wait_ge(T.sem.sent, sent[0])
 
     e_one, e_zero, e_w2, e_oq, e_q = ev(), ev(), ev(), ev(), ev()
@@ -162,6 +185,7 @@ def rank_program(g, core, T, topo):
         stores[0] += 16
 
     Y.wait_ge(e_w2, 1)
+    store(T.w[1:2, :], T.wone[0:1, :])
     store(T.w[2:3, :], T.wone[0:1, :])
 
     e_st = [[ev(), ev()] for _ in range(NB)]
@@ -170,13 +194,15 @@ def rank_program(g, core, T, topo):
     e_r = [[ev(), ev()] for _ in range(NB)]
 
     P.wait_ge(e_q, 1)
-    for i in range(NB):
+    P.wait_ge(LP, 48)
+
+    def scores(i):
         bc, bs = T["bc%d" % i], T["bs%d" % i]
         for h in range(2):
             if i == 0:
-                P.wait_ge(LA if h == 0 else LB, 32 if h == 0 else 64)
+                P.wait_ge(LA if h == 0 else LB, 16 if h == 0 else 32)
             else:
-                P.wait_ge(T.sem["a%d%d" % (i, h)], 2 * NENG)
+                P.wait_ge(T.sem["a%d%d" % (i, h)], arrive[(i, h)])
                 P.wait_ge(e_r[i - 1][h], 1)
             k = STCOL[h]
             P.matmul_mx(T.pst[:, 512 * h:512 * h + 256], T.qc[:], T.qs[:], bc[:, k:k + 256], bs[:, k:k + 256],
@@ -187,6 +213,14 @@ def rank_program(g, core, T, topo):
                 k = KCOL[b]
                 P.matmul_mx(T.pss[:, 512 * b:512 * b + 128], bc[:, k:k + 128], bs[:, k:k + 128], T.qc[:], T.qs[:],
                             True, True).then_inc(e_s[i][b], 1)
+
+    def products(i, e_in, ol, oa, start, stop):
+        pc, pp = T["pc%d" % i], T["pp%d" % i]
+        P.wait_ge(e_in, 1)
+        ml = P.matmul_mx(ol, T.onec[:], T.ones[:], pc[:], pp[:], start, stop)
+        ma = P.matmul_mx(oa, T["bc%d" % i][:, VCOL:VCOL + 128], T["bs%d" % i][:, VCOL:VCOL + 128], pc[:], pp[:],
+                         start, stop)
+        return ml, ma
 
     def scale_and_max(i):
         t = T["t%d" % i]
@@ -215,65 +249,78 @@ def rank_program(g, core, T, topo):
         S.activation(c[64:128, 0:64], c[0:64, 0:64], AF.Copy).then_inc(e2, 1)
         return e2
 
+    scores(0)
     scale_and_max(0)
-    scale_and_max(1)
-    e_m, e_z = ev(), ev()
-    for i in range(2):
-        for h in range(2):
-            V.wait_ge(e_r[i][h], 1)
-    V.tensor_reduce(T.mc[:, 0:1], T.red[:, 0:4], AxisListType.X, OP.max).then_inc(e_m, 1)
+    e_m, e_zr, e_z = ev(), ev(), ev()
+    V.wait_ge(e_r[0][0], 1)
+    V.wait_ge(e_r[0][1], 1)
+    V.tensor_reduce(T.mc[:, 0:1], T.red[:, 0:2], AxisListType.X, OP.max).then_inc(e_m, 1)
     V.wait_ge(e_m, 1)
     V.wait_ge(e_zero, 1)
     V.tensor_scalar(T.z01[:], T.zero[:], T.mc[:, 0:1], SCALE, OP.add, OP.mult).then_inc(e_z, 1)
+    V.tensor_scalar(T.z0r[:], T.zero[:], T.mc[:, 0:1], None, OP.add).then_inc(e_zr, 1)
     e_c01 = spread(T.z01, T.c01, e_z)
     Y.wait_ge(e_c01, 2)
     store(T.c[0:1, :], T.c01[0:1, :])
-    store(T.c[1:2, :], T.c01[0:1, :])
     V.wait_ge(e_c01, 2)
-    e_sub, e_exp, e_p, e_pq = [ev(), ev()], [ev(), ev()], [ev(), ev()], [ev(), ev()]
-    for i in range(2):
-        t = T["t%d" % i]
-        for b in range(4):
-            V.wait_ge(e_t[i][b], 1)
-            V.tensor_tensor(t[:, b:512:4], t[:, b:512:4], T.c01[:], OP.subtract).then_inc(e_sub[i], 1)
-        S.wait_ge(e_sub[i], 4)
-        S.activation(T["pt%d" % i][:], t[:], AF.Exp).then_inc(e_exp[i], 1)
+    e_sub0, e_exp0, e_p0, e_pq0 = ev(), ev(), ev(), ev()
+    for b in range(4):
+        V.wait_ge(e_t[0][b], 1)
+        V.tensor_tensor(T.t0[:, b:512:4], T.t0[:, b:512:4], T.c01[:], OP.subtract).then_inc(e_sub0, 1)
+    S.wait_ge(e_sub0, 4)
+    S.activation(T.pt0[:], T.t0[:], AF.Exp).then_inc(e_exp0, 1)
+    V.wait_ge(e_exp0, 1)
+    V.tensor_scalar(T.pt0[:], T.pt0[:], FLOOR, None, OP.max).then_inc(e_p0, 1)
+    V.wait_ge(e_p0, 1)
+    V.quantize_mx(T.pc0[:], T.pp0[:], T.pt0[:]).then_inc(e_pq0, 1)
+    Y.wait_ge(e_p0, 1)
+    store(T.p[0], T.pt0[:])
     e_l01, e_a01 = ev(), ev()
     P.wait_ge(e_oq, 1)
-    for i in range(2):
-        pt, pc, pp = T["pt%d" % i], T["pc%d" % i], T["pp%d" % i]
-        V.wait_ge(e_exp[i], 1)
-        V.tensor_scalar(pt[:], pt[:], FLOOR, None, OP.max).then_inc(e_p[i], 1)
-        V.wait_ge(e_p[i], 1)
-        V.quantize_mx(pc[:], pp[:], pt[:]).then_inc(e_pq[i], 1)
-        Y.wait_ge(e_p[i], 1)
-        store(T.p[i], pt[:])
-        P.wait_ge(e_pq[i], 1)
-        ml = P.matmul_mx(T.psl[:, 0:128], T.onec[:], T.ones[:], pc[:], pp[:], i == 0, i == 1)
-        ma = P.matmul_mx(T.psa[:, 0:128], T["bc%d" % i][:, VCOL:VCOL + 128], T["bs%d" % i][:, VCOL:VCOL + 128],
-                         pc[:], pp[:], i == 0, i == 1)
-        if i == 1:
-            ml.then_inc(e_l01, 1)
-            ma.then_inc(e_a01, 1)
+    ml, ma = products(0, e_pq0, T.psl[:, 0:128], T.psa[:, 0:128], True, True)
+    ml.then_inc(e_l01, 1)
+    ma.then_inc(e_a01, 1)
 
+    scores(1)
+    scores(2)
+    scale_and_max(1)
     scale_and_max(2)
     e_m2, e_z2 = ev(), ev()
-    V.wait_ge(e_r[2][0], 1)
-    V.wait_ge(e_r[2][1], 1)
-    V.tensor_scalar(T.mc[:, 1:2], T.red[:, 4:5], T.red[:, 5:6], SCALE, OP.max, OP.mult).then_inc(e_m2, 1)
+    for i in (1, 2):
+        V.wait_ge(e_r[i][0], 1)
+        V.wait_ge(e_r[i][1], 1)
+    V.tensor_reduce(T.mc[:, 1:2], T.red[:, 2:6], AxisListType.X, OP.max).then_inc(e_m2, 1)
     V.wait_ge(e_m2, 1)
-    V.tensor_scalar(T.z2[:], T.z01[:], T.mc[:, 1:2], None, OP.max).then_inc(e_z2, 1)
+    V.wait_ge(e_zr, 1)
+    V.tensor_scalar(T.z2[:], T.z0r[:], T.mc[:, 1:2], SCALE, OP.max, OP.mult).then_inc(e_z2, 1)
     e_c2 = spread(T.z2, T.c2, e_z2)
     Y.wait_ge(e_c2, 2)
+    store(T.c[1:2, :], T.c2[0:1, :])
     store(T.c[2:3, :], T.c2[0:1, :])
     V.wait_ge(e_c2, 2)
-    e_sb, e_ex = [ev() for _ in range(4)], [ev() for _ in range(4)]
-    e_p2, e_pq2 = ev(), ev()
+    e_sb = [[ev() for _ in range(4)] for _ in range(2)]
+    e_ex1, e_ex = ev(), [ev() for _ in range(4)]
+    e_p1, e_pq1, e_p2, e_pq2 = ev(), ev(), ev(), ev()
+
+    def shift_exp(i, b):
+        t, pt = T["t%d" % i], T["pt%d" % i]
+        V.wait_ge(e_t[i][b], 1)
+        V.tensor_tensor(t[:, b:512:4], t[:, b:512:4], T.c2[:], OP.subtract).then_inc(e_sb[i - 1][b], 1)
+        S.wait_ge(e_sb[i - 1][b], 1)
+        S.activation(pt[:, b:512:4], t[:, b:512:4], AF.Exp).then_inc(e_ex1 if i == 1 else e_ex[b], 1)
+
     for b in range(4):
-        V.wait_ge(e_t[2][b], 1)
-        V.tensor_tensor(T.t2[:, b:512:4], T.t2[:, b:512:4], T.c2[:], OP.subtract).then_inc(e_sb[b], 1)
-        S.wait_ge(e_sb[b], 1)
-        S.activation(T.pt2[:, b:512:4], T.t2[:, b:512:4], AF.Exp).then_inc(e_ex[b], 1)
+        shift_exp(1, b)
+    shift_exp(2, 0)
+    shift_exp(2, 1)
+    V.wait_ge(e_ex1, 4)
+    V.tensor_scalar(T.pt1[:], T.pt1[:], FLOOR, None, OP.max).then_inc(e_p1, 1)
+    V.wait_ge(e_p1, 1)
+    V.quantize_mx(T.pc1[:], T.pp1[:], T.pt1[:]).then_inc(e_pq1, 1)
+    Y.wait_ge(e_p1, 1)
+    store(T.p[1], T.pt1[:])
+    shift_exp(2, 2)
+    shift_exp(2, 3)
     for b in range(4):
         V.wait_ge(e_ex[b], 1)
         V.tensor_scalar(T.pt2[:, b:512:4], T.pt2[:, b:512:4], FLOOR, None, OP.max).then_inc(e_p2, 1)
@@ -282,10 +329,10 @@ def rank_program(g, core, T, topo):
     Y.wait_ge(e_p2, 4)
     store(T.p[2], T.pt2[:])
     e_l2, e_a2 = ev(), ev()
-    P.wait_ge(e_pq2, 1)
-    P.matmul_mx(T.pst[:, 0:128], T.onec[:], T.ones[:], T.pc2[:], T.pp2[:], True, True).then_inc(e_l2, 1)
-    P.matmul_mx(T.pst[:, 512:640], T.bc2[:, VCOL:VCOL + 128], T.bs2[:, VCOL:VCOL + 128], T.pc2[:], T.pp2[:],
-                True, True).then_inc(e_a2, 1)
+    products(1, e_pq1, T.pst[:, 0:128], T.pst[:, 512:640], True, False)
+    ml, ma = products(2, e_pq2, T.pst[:, 0:128], T.pst[:, 512:640], False, True)
+    ml.then_inc(e_l2, 1)
+    ma.then_inc(e_a2, 1)
 
     e_dc, e_al, e_td, e_tn, e_den, e_rd, e_num, e_o = ev(), ev(), ev(), ev(), ev(), ev(), ev(), ev()
     V.tensor_tensor(T.dc[:], T.c01[:], T.c2[:], OP.subtract).then_inc(e_dc, 1)
@@ -293,7 +340,6 @@ def rank_program(g, core, T, topo):
     S.activation(T.al[:], T.dc[:], AF.Exp).then_inc(e_al, 1)
     Y.wait_ge(e_al, 1)
     store(T.w[0:1, :], T.al[0:1, :])
-    store(T.w[1:2, :], T.al[0:1, :])
     V.wait_ge(e_al, 1)
     V.wait_ge(e_l01, 1)
     V.tensor_tensor(T.td[:], T.psl[:, 0:128], T.al[:], OP.mult).then_inc(e_td, 1)

@@ -7,7 +7,8 @@ NB = 3
 SCALE = 0.0125
 FLOOR = math.exp(-20.0)
 W = 640
-HALF = ((0, 320), (320, 640))
+QUART = ((0, 160), (160, 320), (320, 480), (480, 640))
+PLANE = (("k", 0), ("v", 0), ("k", 1), ("v", 1))
 KCOL = (0, 128, 384, 512)
 VCOL = 256
 STCOL = (0, 384)
@@ -20,21 +21,28 @@ SCRATCH = {
     "onet": ("sbuf", [128, 512], "bfloat16"),
     "onec": ("sbuf", [128, 128], "float8_e4m3fn_x4"),
     "ones": ("sbuf", [128, 128], "uint8"),
-    "rc": ("sbuf", [128, 320], "float8_e4m3fn_x4"),
-    "rs": ("sbuf", [128, 320], "uint8"),
+    "rc": ("sbuf", [128, 160], "float8_e4m3fn_x4"),
+    "dk": ("dram", [128, 512], "uint8"),
+    "dv": ("dram", [128, 128], "uint8"),
+    "dk1": ("dram", [128, 512], "uint8"),
+    "dv1": ("dram", [128, 128], "uint8"),
+    "dk2": ("dram", [128, 512], "uint8"),
+    "dv2": ("dram", [128, 128], "uint8"),
     "zero": ("sbuf", [128, 128], "float32"),
     "wone": ("sbuf", [128, 128], "float32"),
     "red": ("sbuf", [128, 8], "float32"),
     "mc": ("sbuf", [128, 4], "float32"),
+    "md": ("sbuf", [128, 4], "float32"),
     "z01": ("sbuf", [128, 128], "float32"),
     "z0r": ("sbuf", [128, 128], "float32"),
+    "z1r": ("sbuf", [128, 128], "float32"),
+    "z2a": ("sbuf", [128, 128], "float32"),
     "z2": ("sbuf", [128, 128], "float32"),
     "c01": ("sbuf", [128, 128], "float32"),
     "c2": ("sbuf", [128, 128], "float32"),
     "dc": ("sbuf", [128, 128], "float32"),
     "al": ("sbuf", [128, 128], "float32"),
     "tn": ("sbuf", [128, 128], "float32"),
-    "td": ("sbuf", [128, 128], "float32"),
     "den": ("sbuf", [128, 128], "float32"),
     "rd": ("sbuf", [128, 128], "float32"),
     "num": ("sbuf", [128, 128], "float32"),
@@ -52,13 +60,15 @@ for _i in range(NB):
     SCRATCH["pc%d" % _i] = ("sbuf", [128, 128], "float8_e4m3fn_x4")
     SCRATCH["pp%d" % _i] = ("sbuf", [128, 128], "uint8")
 
-SEMAPHORES = (["la", "lb", "lp", "lq", "st", "rinp", "rinc", "sent", "a10", "a11", "a20", "a21"]
-              + ["e%d" % _k for _k in range(NEV)])
+SEMAPHORES = (["la", "lb", "lp", "ls", "lq", "st", "rinp", "rinc", "sent", "a10", "a11", "a20", "a21",
+               "k1", "k2", "v1", "v2", "pl1", "pl2"] + ["e%d" % _k for _k in range(NEV)])
 
 
 def _split(mask, k):
     eng = [e for e in range(16) if (mask >> e) & 1]
-    n = len(eng) // k
+    n = 1
+    while 2 * n * k <= len(eng):
+        n *= 2
     return [sum(1 << e for e in eng[i * n:(i + 1) * n]) for i in range(k)], n
 
 
@@ -69,22 +79,18 @@ def _plan(T, topo):
     for j, cj in enumerate(cores):
         dests = [(cores[(j + i) % n], i) for i in range(1, NB)]
         mates = [c for c in range(NSIM) if topo.chip(c) == topo.chip(cj) and c != cj and T.rank_of(c) is None]
-        pools = {0: [c for c in mates if topo.die(c) == topo.die(cj)],
-                 1: [c for c in mates if topo.die(c) != topo.die(cj)]}
-        used = []
-        feeds = {0: [], 1: []}
-        for h in (1, 0):
-            for d in dests:
-                if h == 0 and cj not in used and topo.may_write(cj, d[0]):
-                    r = cj
-                else:
-                    r = [c for c in pools[h] if c not in used and topo.may_write(c, d[0])][0]
-                    feeds[h].append(r)
-                used.append(r)
-                groups.append((r, h, [d]))
+        feeds = []
         for h in (0, 1):
-            for r in feeds[h]:
-                jobs[r] = ("relay", cj, len(feeds[h]))
+            pool = [cj] if h == 0 else []
+            pool += [c for c in mates if (topo.die(c) == topo.die(cj)) == (h == 0)]
+            pool = [c for c in pool if all(topo.may_write(c, d[0]) for d in dests)]
+            for i in range(2):
+                groups.append((pool[i], 2 * h + i, dests))
+                if pool[i] != cj:
+                    feeds.append((pool[i], 2 * h + i))
+        for r, q in feeds:
+            jobs[r] = ("relay", cj, len([1 for _, x in feeds if PLANE[x][0] == PLANE[q][0]]),
+                       len([1 for _, x in feeds if x // 2 == q // 2]))
         jobs[cj] = ("rank", feeds)
     return jobs, groups
 
@@ -98,10 +104,12 @@ def rank_program(g, core, T, topo):
     sent = [0]
     mine = [gr for gr in groups if gr[0] == core]
 
-    def send(targets, src, codes):
+    def send(targets, codes):
+        if not targets:
+            return
         masks, n = _split(topo.mask(core, targets[0][0]), len(targets))
         trs = []
-        for (dst, out, sem), m in zip(targets, masks):
+        for (dst, out, sem, src), m in zip(targets, masks):
             rid, pid, _ = topo.addr(dst)
             trs.append(RemoteDMATransfer(dst_ids=[DstId(rid=rid, pnc=pid)], dma_engine_mask=m, remote_sem=sem,
                                          src=src.bitcast(u8) if codes else src,
@@ -109,22 +117,22 @@ def rank_program(g, core, T, topo):
             sent[0] += n
         g.remote_dma_fused(trs, local_sem=T.sem.sent)
 
-    def planes_out(src):
-        for _, h, dests in mine:
-            a, b = HALF[h]
-            send([(d, T["bs%d" % k][:, a:b], T.sem["a%d%d" % (k, h)]) for d, k in dests], src, False)
+    def plane_out():
+        for _, q, dests in mine:
+            w, i = PLANE[q]
+            d, k = dests[i]
+            send([(d, T["d%s%d" % (w, k)][:], T.sem["%s%d" % (w, k)], T["d" + w][:])], False)
 
     def codes_out(src):
-        for _, h, dests in mine:
-            a, b = HALF[h]
+        for _, q, dests in mine:
+            a, b = QUART[q]
             for d, k in dests:
-                send([(d, T["bc%d" % k][:, a:b], T.sem["a%d%d" % (k, h)])], src, True)
+                send([(d, T["bc%d" % k][:, a:b], T.sem["a%d%d" % (k, q // 2)], src)], True)
 
     if job[0] == "relay":
-        nfeed = _split(topo.mask(job[1], core), job[2])[1]
-        g.wait_ge(T.sem.rinp, nfeed)
-        planes_out(T.rs[:])
-        g.wait_ge(T.sem.rinc, nfeed)
+        g.wait_ge(T.sem.rinp, _split(topo.mask(job[1], core), job[2])[1])
+        plane_out()
+        g.wait_ge(T.sem.rinc, _split(topo.mask(job[1], core), job[3])[1])
         codes_out(T.rc[:])
         g.wait_ge(T.sem.sent, sent[0])
         return
@@ -139,34 +147,39 @@ def rank_program(g, core, T, topo):
         nev[0] += 1
         return s
 
-    arrive = {}
-    for snd, h, dests in groups:
-        for d, k in dests:
+    arrive, plane_in = {}, {}
+    for snd, q, dests in groups:
+        for i, (d, k) in enumerate(dests):
             if d == core:
-                arrive[(k, h)] = _split(topo.mask(snd, d), len(dests))[1] + _split(topo.mask(snd, d), 1)[1]
+                n = _split(topo.mask(snd, d), 1)[1]
+                arrive[(k, q // 2)] = arrive.get((k, q // 2), 0) + n
+                if PLANE[q][1] == i:
+                    plane_in[(PLANE[q][0], k)] = n
 
-    LA, LB, LP, LQ = T.sem.la, T.sem.lb, T.sem.lp, T.sem.lq
-    S.dma_start(T.bs0[:, 384:640], T.ks[:, 256:512]).then_inc(LP, 16)
-    S.dma_start(T.bs0[:, 256:384], T.vs[:]).then_inc(LP, 16)
-    S.dma_start(T.bs0[:, 0:256], T.ks[:, 0:256]).then_inc(LP, 16)
+    LA, LB, LP, LS, LQ = T.sem.la, T.sem.lb, T.sem.lp, T.sem.ls, T.sem.lq
+    S.dma_start(T.dk[:], T.ks[:]).then_inc(LP, 16)
+    S.dma_start(T.dv[:], T.vs[:]).then_inc(LP, 16)
     Y.dma_start(T.bc0[:, 384:640].bitcast(u8), T.kc[:, 1024:2048]).then_inc(LB, 16)
     Y.dma_start(T.bc0[:, 256:384].bitcast(u8), T.vc[:]).then_inc(LB, 16)
     Y.dma_start(T.bc0[:, 0:256].bitcast(u8), T.kc[:, 0:1024]).then_inc(LA, 16)
+    S.dma_start(T.bs0[:, 384:640], T.ks[:, 256:512]).then_inc(LS, 16)
+    S.dma_start(T.bs0[:, 256:384], T.vs[:]).then_inc(LS, 16)
+    S.dma_start(T.bs0[:, 0:256], T.ks[:, 0:256]).then_inc(LS, 16)
     S.dma_start(T.qt[:], T.q[:]).then_inc(LQ, 16)
 
-    a0, b0 = HALF[0]
-    a1, b1 = HALF[1]
-    g.wait_ge(LP, 48)
-    send([(r, T.rs[:], T.sem.rinp) for r in feeds[1]], T.bs0[:, a1:b1], False)
-    if feeds[0]:
-        send([(r, T.rs[:], T.sem.rinp) for r in feeds[0]], T.bs0[:, a0:b0], False)
-    planes_out(T.bs0[:, a0:b0])
+    def cols(t, q):
+        return t[:, QUART[q][0]:QUART[q][1]]
+
+    g.wait_ge(LP, 32)
+    for w in ("k", "v"):
+        send([(r, T["d" + w][:], T.sem.rinp, T["d" + w][:]) for r, q in feeds if PLANE[q][0] == w], False)
+    plane_out()
     g.wait_ge(LB, 32)
-    send([(r, T.rc[:], T.sem.rinc) for r in feeds[1]], T.bc0[:, a1:b1], True)
+    send([(r, T.rc[:], T.sem.rinc, cols(T.bc0, q)) for r, q in feeds if q // 2 == 1], True)
     g.wait_ge(LA, 16)
-    if feeds[0]:
-        send([(r, T.rc[:], T.sem.rinc) for r in feeds[0]], T.bc0[:, a0:b0], True)
-    codes_out(T.bc0[:, a0:b0])
+    send([(r, T.rc[:], T.sem.rinc, cols(T.bc0, q)) for r, q in feeds if q // 2 == 0], True)
+    for _, q, _ in mine:
+        codes_out(cols(T.bc0, q))
     g.wait_ge(T.sem.sent, sent[0])
 
     e_one, e_zero, e_w2, e_oq, e_q = ev(), ev(), ev(), ev(), ev()
@@ -188,16 +201,26 @@ def rank_program(g, core, T, topo):
     store(T.w[1:2, :], T.wone[0:1, :])
     store(T.w[2:3, :], T.wone[0:1, :])
 
+    for k in range(1, NB):
+        bs, pl = T["bs%d" % k], T.sem["pl%d" % k]
+        Y.wait_ge(T.sem["k%d" % k], plane_in[("k", k)])
+        Y.dma_start(bs[:, 0:256], T["dk%d" % k][:, 0:256]).then_inc(pl, 16)
+        Y.dma_start(bs[:, 384:640], T["dk%d" % k][:, 256:512]).then_inc(pl, 16)
+        Y.wait_ge(T.sem["v%d" % k], plane_in[("v", k)])
+        Y.dma_start(bs[:, 256:384], T["dv%d" % k][:]).then_inc(pl, 16)
+
     e_st = [[ev(), ev()] for _ in range(NB)]
     e_s = [[ev() for _ in range(4)] for _ in range(NB)]
     e_t = [[ev() for _ in range(4)] for _ in range(NB)]
     e_r = [[ev(), ev()] for _ in range(NB)]
 
     P.wait_ge(e_q, 1)
-    P.wait_ge(LP, 48)
+    P.wait_ge(LS, 48)
 
     def scores(i):
         bc, bs = T["bc%d" % i], T["bs%d" % i]
+        if i > 0:
+            P.wait_ge(T.sem["pl%d" % i], 48)
         for h in range(2):
             if i == 0:
                 P.wait_ge(LA if h == 0 else LB, 16 if h == 0 else 32)
@@ -207,17 +230,17 @@ def rank_program(g, core, T, topo):
             k = STCOL[h]
             P.matmul_mx(T.pst[:, 512 * h:512 * h + 256], T.qc[:], T.qs[:], bc[:, k:k + 256], bs[:, k:k + 256],
                         True, True).then_inc(e_st[i][h], 1)
-            for b in (2 * h, 2 * h + 1):
-                if i > 0:
-                    P.wait_ge(e_t[i - 1][b], 1)
-                k = KCOL[b]
-                P.matmul_mx(T.pss[:, 512 * b:512 * b + 128], bc[:, k:k + 128], bs[:, k:k + 128], T.qc[:], T.qs[:],
-                            True, True).then_inc(e_s[i][b], 1)
+        for b in range(4):
+            if i > 0:
+                P.wait_ge(e_t[i - 1][b], 1)
+            k = KCOL[b]
+            P.matmul_mx(T.pss[:, 512 * b:512 * b + 128], bc[:, k:k + 128], bs[:, k:k + 128], T.qc[:], T.qs[:],
+                        True, True).then_inc(e_s[i][b], 1)
 
     def products(i, e_in, ol, oa, start, stop):
         pc, pp = T["pc%d" % i], T["pp%d" % i]
         P.wait_ge(e_in, 1)
-        ml = P.matmul_mx(ol, T.onec[:], T.ones[:], pc[:], pp[:], start, stop)
+        ml = P.matmul_mx(ol, pc[:], pp[:], T.onec[:], T.ones[:], start, stop)
         ma = P.matmul_mx(oa, T["bc%d" % i][:, VCOL:VCOL + 128], T["bs%d" % i][:, VCOL:VCOL + 128], pc[:], pp[:],
                          start, stop)
         return ml, ma
@@ -228,10 +251,10 @@ def rank_program(g, core, T, topo):
             V.wait_ge(e_st[i][h], 1)
             V.tensor_reduce(T.red[:, 2 * i + h:2 * i + h + 1], T.pst[:, 512 * h:512 * h + 256], AxisListType.X,
                             OP.max).then_inc(e_r[i][h], 1)
-            for b in (2 * h, 2 * h + 1):
-                S.wait_ge(e_s[i][b], 1)
-                S.activation(t[:, b:512:4], T.pss[:, 512 * b:512 * b + 128], AF.Identity,
-                             scale=SCALE).then_inc(e_t[i][b], 1)
+        for b in range(4):
+            S.wait_ge(e_s[i][b], 1)
+            S.activation(t[:, b:512:4], T.pss[:, 512 * b:512 * b + 128], AF.Identity,
+                         scale=SCALE).then_inc(e_t[i][b], 1)
 
     def spread(z, c, e_z):
         e_x, e1, e2 = ev(), ev(), ev()
@@ -280,19 +303,25 @@ def rank_program(g, core, T, topo):
     ml, ma = products(0, e_pq0, T.psl[:, 0:128], T.psa[:, 0:128], True, True)
     ml.then_inc(e_l01, 1)
     ma.then_inc(e_a01, 1)
+    e_l0 = ev()
+    V.wait_ge(e_l01, 1)
+    V.tensor_copy(T.mc[:, 2:3], T.psl[:, 0:1]).then_inc(e_l0, 1)
 
     scores(1)
     scores(2)
     scale_and_max(1)
-    scale_and_max(2)
-    e_m2, e_z2 = ev(), ev()
-    for i in (1, 2):
-        V.wait_ge(e_r[i][0], 1)
-        V.wait_ge(e_r[i][1], 1)
-    V.tensor_reduce(T.mc[:, 1:2], T.red[:, 2:6], AxisListType.X, OP.max).then_inc(e_m2, 1)
-    V.wait_ge(e_m2, 1)
+    e_z1, e_za, e_z2 = ev(), ev(), ev()
+    V.wait_ge(e_r[1][0], 1)
+    V.wait_ge(e_r[1][1], 1)
     V.wait_ge(e_zr, 1)
-    V.tensor_scalar(T.z2[:], T.z0r[:], T.mc[:, 1:2], SCALE, OP.max, OP.mult).then_inc(e_z2, 1)
+    V.tensor_scalar(T.z1r[:], T.z0r[:], T.red[:, 2:3], T.red[:, 3:4], OP.max, OP.max).then_inc(e_z1, 1)
+    scale_and_max(2)
+    V.wait_ge(e_z1, 1)
+    V.wait_ge(e_r[2][0], 1)
+    V.tensor_scalar(T.z2a[:], T.z1r[:], T.red[:, 4:5], None, OP.max).then_inc(e_za, 1)
+    V.wait_ge(e_za, 1)
+    V.wait_ge(e_r[2][1], 1)
+    V.tensor_scalar(T.z2[:], T.z2a[:], T.red[:, 5:6], SCALE, OP.max, OP.mult).then_inc(e_z2, 1)
     e_c2 = spread(T.z2, T.c2, e_z2)
     Y.wait_ge(e_c2, 2)
     store(T.c[1:2, :], T.c2[0:1, :])
@@ -334,26 +363,31 @@ def rank_program(g, core, T, topo):
     ml.then_inc(e_l2, 1)
     ma.then_inc(e_a2, 1)
 
-    e_dc, e_al, e_td, e_tn, e_den, e_rd, e_num, e_o = ev(), ev(), ev(), ev(), ev(), ev(), ev(), ev()
+    e_dk, e_ak, e_dc, e_al, e_tn, e_den, e_rd, e_zq, e_num, e_o = [ev() for _ in range(10)]
+    V.tensor_tensor(T.mc[:, 3:4], T.z01[:, 0:1], T.z2[:, 0:1], OP.subtract).then_inc(e_dk, 1)
     V.tensor_tensor(T.dc[:], T.c01[:], T.c2[:], OP.subtract).then_inc(e_dc, 1)
+    S.wait_ge(e_dk, 1)
+    S.activation(T.md[:, 0:1], T.mc[:, 3:4], AF.Exp).then_inc(e_ak, 1)
     S.wait_ge(e_dc, 1)
     S.activation(T.al[:], T.dc[:], AF.Exp).then_inc(e_al, 1)
     Y.wait_ge(e_al, 1)
     store(T.w[0:1, :], T.al[0:1, :])
+    V.wait_ge(e_ak, 1)
+    V.wait_ge(e_l0, 1)
+    V.wait_ge(e_l2, 1)
+    V.tensor_scalar(T.md[:, 1:2], T.mc[:, 2:3], T.md[:, 0:1], T.pst[:, 0:1], OP.mult, OP.add).then_inc(e_den, 1)
+    V.wait_ge(e_den, 1)
+    V.reciprocal(T.md[:, 2:3], T.md[:, 1:2]).then_inc(e_rd, 1)
+    V.wait_ge(e_rd, 1)
+    V.tensor_scalar(T.den[:], T.zero[:], T.md[:, 2:3], None, OP.add).then_inc(e_zq, 1)
     V.wait_ge(e_al, 1)
-    V.wait_ge(e_l01, 1)
-    V.tensor_tensor(T.td[:], T.psl[:, 0:128], T.al[:], OP.mult).then_inc(e_td, 1)
     V.wait_ge(e_a01, 1)
     V.tensor_tensor(T.tn[:], T.psa[:, 0:128], T.al[:], OP.mult).then_inc(e_tn, 1)
-    V.wait_ge(e_td, 1)
-    V.wait_ge(e_l2, 1)
-    V.tensor_tensor(T.den[:], T.pst[:, 0:128], T.td[:], OP.add).then_inc(e_den, 1)
-    V.wait_ge(e_den, 1)
-    V.reciprocal(T.rd[:], T.den[:]).then_inc(e_rd, 1)
+    e_r2 = spread(T.den, T.rd, e_zq)
     V.wait_ge(e_tn, 1)
     V.wait_ge(e_a2, 1)
     V.tensor_tensor(T.num[:], T.pst[:, 512:640], T.tn[:], OP.add).then_inc(e_num, 1)
-    V.wait_ge(e_rd, 1)
+    V.wait_ge(e_r2, 2)
     V.wait_ge(e_num, 1)
     V.tensor_tensor(T.ot[:], T.num[:], T.rd[:], OP.mult).then_inc(e_o, 1)
     Y.wait_ge(e_o, 1)

@@ -61,7 +61,7 @@ for _i in range(NB):
     SCRATCH["pp%d" % _i] = ("sbuf", [128, 128], "uint8")
 
 SEMAPHORES = (["la", "lb", "lp", "ls", "lq", "st", "rinp", "rinc", "sent", "a10", "a11", "a20", "a21",
-               "k1", "k2", "v1", "v2", "pl1", "pl2"] + ["e%d" % _k for _k in range(NEV)])
+               "k1", "k2", "v1", "v2", "pl1", "pl2", "one"] + ["e%d" % _k for _k in range(NEV)])
 
 
 def _split(mask, k):
@@ -70,6 +70,14 @@ def _split(mask, k):
     while 2 * n * k <= len(eng):
         n *= 2
     return [sum(1 << e for e in eng[i * n:(i + 1) * n]) for i in range(k)], n
+
+
+def _one_cols(k, n):
+    return (128 * k // n) // 4 * 4, (128 * (k + 1) // n) // 4 * 4
+
+
+def _one_mask(topo, helper, rank_core, dest):
+    return topo.mask(helper, rank_core) & topo.mask(helper, dest)
 
 
 def _plan(T, topo):
@@ -104,10 +112,10 @@ def rank_program(g, core, T, topo):
     sent = [0]
     mine = [gr for gr in groups if gr[0] == core]
 
-    def send(targets, codes):
+    def send(targets, codes, mask=None):
         if not targets:
             return
-        masks, n = _split(topo.mask(core, targets[0][0]), len(targets))
+        masks, n = _split(topo.mask(core, targets[0][0]) if mask is None else mask, len(targets))
         trs = []
         for (dst, out, sem, src), m in zip(targets, masks):
             rid, pid, _ = topo.addr(dst)
@@ -130,6 +138,15 @@ def rank_program(g, core, T, topo):
                 send([(d, T["bc%d" % k][:, a:b], T.sem["a%d%d" % (k, q // 2)], src)], True)
 
     if job[0] == "relay":
+        hs = [r for r, _ in jobs[job[1]][1]]
+        a, b = _one_cols(hs.index(core), len(hs))
+        g.vector.memset(T.onet[:], 1.0).then_inc(T.sem.e0, 1)
+        g.vector.wait_ge(T.sem.e0, 1)
+        g.vector.quantize_mx(T.onec[:], T.ones[:], T.onet[:]).then_inc(T.sem.e1, 1)
+        g.wait_ge(T.sem.e1, 1)
+        m = _one_mask(topo, core, job[1], mine[0][2][0][0])
+        send([(job[1], T.onec[:, a:b], T.sem.one, T.onec[:, a:b])], True, m)
+        send([(job[1], T.ones[:, a:b], T.sem.one, T.ones[:, a:b])], False, m)
         g.wait_ge(T.sem.rinp, _split(topo.mask(job[1], core), job[2])[1])
         plane_out()
         g.wait_ge(T.sem.rinc, _split(topo.mask(job[1], core), job[3])[1])
@@ -155,17 +172,20 @@ def rank_program(g, core, T, topo):
                 arrive[(k, q // 2)] = arrive.get((k, q // 2), 0) + n
                 if PLANE[q][1] == i:
                     plane_in[(PLANE[q][0], k)] = n
+    one_in = 0
+    for snd, q, dests in groups:
+        if (snd, q) in feeds:
+            one_in += 2 * _split(_one_mask(topo, snd, core, dests[0][0]), 1)[1]
 
     LA, LB, LP, LS, LQ = T.sem.la, T.sem.lb, T.sem.lp, T.sem.ls, T.sem.lq
     S.dma_start(T.dk[:], T.ks[:]).then_inc(LP, 16)
-    S.dma_start(T.dv[:], T.vs[:]).then_inc(LP, 16)
+    Y.dma_start(T.dv[:], T.vs[:]).then_inc(LP, 16)
     Y.dma_start(T.bc0[:, 384:640].bitcast(u8), T.kc[:, 1024:2048]).then_inc(LB, 16)
-    Y.dma_start(T.bc0[:, 256:384].bitcast(u8), T.vc[:]).then_inc(LB, 16)
+    S.dma_start(T.bc0[:, 256:384].bitcast(u8), T.vc[:]).then_inc(LB, 16)
     Y.dma_start(T.bc0[:, 0:256].bitcast(u8), T.kc[:, 0:1024]).then_inc(LA, 16)
-    S.dma_start(T.bs0[:, 384:640], T.ks[:, 256:512]).then_inc(LS, 16)
-    S.dma_start(T.bs0[:, 256:384], T.vs[:]).then_inc(LS, 16)
-    S.dma_start(T.bs0[:, 0:256], T.ks[:, 0:256]).then_inc(LS, 16)
     S.dma_start(T.qt[:], T.q[:]).then_inc(LQ, 16)
+    S.dma_start(T.bs0[:, 0:512], T.ks[:]).then_inc(LS, 16)
+    Y.dma_start(T.bs0[:, 512:640], T.vs[:]).then_inc(LS, 16)
 
     def cols(t, q):
         return t[:, QUART[q][0]:QUART[q][1]]
@@ -182,12 +202,9 @@ def rank_program(g, core, T, topo):
         codes_out(cols(T.bc0, q))
     g.wait_ge(T.sem.sent, sent[0])
 
-    e_one, e_zero, e_w2, e_oq, e_q = ev(), ev(), ev(), ev(), ev()
-    V.memset(T.onet[:], 1.0).then_inc(e_one, 1)
+    e_zero, e_w2, e_q = ev(), ev(), ev()
     V.memset(T.zero[:], 0.0).then_inc(e_zero, 1)
     V.memset(T.wone[0:1, :], 1.0).then_inc(e_w2, 1)
-    V.wait_ge(e_one, 1)
-    V.quantize_mx(T.onec[:], T.ones[:], T.onet[:]).then_inc(e_oq, 1)
     V.wait_ge(LQ, 16)
     V.quantize_mx(T.qc[:], T.qs[:], T.qt[:]).then_inc(e_q, 1)
 
@@ -215,7 +232,7 @@ def rank_program(g, core, T, topo):
     e_r = [[ev(), ev()] for _ in range(NB)]
 
     P.wait_ge(e_q, 1)
-    P.wait_ge(LS, 48)
+    P.wait_ge(LS, 32)
 
     def scores(i):
         bc, bs = T["bc%d" % i], T["bs%d" % i]
@@ -227,21 +244,22 @@ def rank_program(g, core, T, topo):
             else:
                 P.wait_ge(T.sem["a%d%d" % (i, h)], arrive[(i, h)])
                 P.wait_ge(e_r[i - 1][h], 1)
-            k = STCOL[h]
-            P.matmul_mx(T.pst[:, 512 * h:512 * h + 256], T.qc[:], T.qs[:], bc[:, k:k + 256], bs[:, k:k + 256],
+            k, kp = STCOL[h], (256 * h if i == 0 else STCOL[h])
+            P.matmul_mx(T.pst[:, 512 * h:512 * h + 256], T.qc[:], T.qs[:], bc[:, k:k + 256], bs[:, kp:kp + 256],
                         True, True).then_inc(e_st[i][h], 1)
         for b in range(4):
             if i > 0:
                 P.wait_ge(e_t[i - 1][b], 1)
-            k = KCOL[b]
-            P.matmul_mx(T.pss[:, 512 * b:512 * b + 128], bc[:, k:k + 128], bs[:, k:k + 128], T.qc[:], T.qs[:],
+            k, kp = KCOL[b], (128 * b if i == 0 else KCOL[b])
+            P.matmul_mx(T.pss[:, 512 * b:512 * b + 128], bc[:, k:k + 128], bs[:, kp:kp + 128], T.qc[:], T.qs[:],
                         True, True).then_inc(e_s[i][b], 1)
 
     def products(i, e_in, ol, oa, start, stop):
         pc, pp = T["pc%d" % i], T["pp%d" % i]
+        vp = 512 if i == 0 else VCOL
         P.wait_ge(e_in, 1)
         ml = P.matmul_mx(ol, pc[:], pp[:], T.onec[:], T.ones[:], start, stop)
-        ma = P.matmul_mx(oa, T["bc%d" % i][:, VCOL:VCOL + 128], T["bs%d" % i][:, VCOL:VCOL + 128], pc[:], pp[:],
+        ma = P.matmul_mx(oa, T["bc%d" % i][:, VCOL:VCOL + 128], T["bs%d" % i][:, vp:vp + 128], pc[:], pp[:],
                          start, stop)
         return ml, ma
 
@@ -299,16 +317,13 @@ def rank_program(g, core, T, topo):
     Y.wait_ge(e_p0, 1)
     store(T.p[0], T.pt0[:])
     e_l01, e_a01 = ev(), ev()
-    P.wait_ge(e_oq, 1)
-    ml, ma = products(0, e_pq0, T.psl[:, 0:128], T.psa[:, 0:128], True, True)
-    ml.then_inc(e_l01, 1)
-    ma.then_inc(e_a01, 1)
-    e_l0 = ev()
-    V.wait_ge(e_l01, 1)
-    V.tensor_copy(T.mc[:, 2:3], T.psl[:, 0:1]).then_inc(e_l0, 1)
 
     scores(1)
     scores(2)
+    P.wait_ge(T.sem.one, one_in)
+    ml, ma = products(0, e_pq0, T.psl[:, 0:128], T.psa[:, 0:128], True, True)
+    ml.then_inc(e_l01, 1)
+    ma.then_inc(e_a01, 1)
     scale_and_max(1)
     e_z1, e_za, e_z2 = ev(), ev(), ev()
     V.wait_ge(e_r[1][0], 1)
@@ -373,9 +388,9 @@ def rank_program(g, core, T, topo):
     Y.wait_ge(e_al, 1)
     store(T.w[0:1, :], T.al[0:1, :])
     V.wait_ge(e_ak, 1)
-    V.wait_ge(e_l0, 1)
+    V.wait_ge(e_l01, 1)
     V.wait_ge(e_l2, 1)
-    V.tensor_scalar(T.md[:, 1:2], T.mc[:, 2:3], T.md[:, 0:1], T.pst[:, 0:1], OP.mult, OP.add).then_inc(e_den, 1)
+    V.tensor_scalar(T.md[:, 1:2], T.psl[:, 0:1], T.md[:, 0:1], T.pst[:, 0:1], OP.mult, OP.add).then_inc(e_den, 1)
     V.wait_ge(e_den, 1)
     V.reciprocal(T.md[:, 2:3], T.md[:, 1:2]).then_inc(e_rd, 1)
     V.wait_ge(e_rd, 1)

import math
from concourse.bass import DstId, RemoteDMATransfer
from concourse.mybir import dt, AluOpType, AxisListType, ActivationFunctionType

NSIM = 128
NB = 3
SCALE = 0.0125
FLOOR = math.exp(-20.0)
W = 640
QUART = ((0, 160), (160, 320), (320, 480), (480, 640))
PLANE = (("k", 0), ("v", 0), ("k", 1), ("v", 1))
KCOL = (0, 128, 384, 512)
VCOL = 256
STCOL = (0, 384)
NEV = 100

SCRATCH = {
    "qt": ("sbuf", [128, 512], "bfloat16"),
    "qc": ("sbuf", [128, 128], "float8_e4m3fn_x4"),
    "qs": ("sbuf", [128, 128], "uint8"),
    "onet": ("sbuf", [128, 512], "bfloat16"),
    "onec": ("sbuf", [128, 128], "float8_e4m3fn_x4"),
    "ones": ("sbuf", [128, 128], "uint8"),
    "rc": ("sbuf", [128, 160], "float8_e4m3fn_x4"),
    "dk": ("dram", [128, 512], "uint8"),
    "dv": ("dram", [128, 128], "uint8"),
    "dk1": ("dram", [128, 512], "uint8"),
    "dv1": ("dram", [128, 128], "uint8"),
    "dk2": ("dram", [128, 512], "uint8"),
    "dv2": ("dram", [128, 128], "uint8"),
    "zero": ("sbuf", [128, 128], "float32"),
    "wone": ("sbuf", [128, 128], "float32"),
    "red": ("sbuf", [128, 8], "float32"),
    "mc": ("sbuf", [128, 4], "float32"),
    "md": ("sbuf", [128, 4], "float32"),
    "z01": ("sbuf", [128, 128], "float32"),
    "z0r": ("sbuf", [128, 128], "float32"),
    "z1r": ("sbuf", [128, 128], "float32"),
    "z2a": ("sbuf", [128, 128], "float32"),
    "z2": ("sbuf", [128, 128], "float32"),
    "c01": ("sbuf", [128, 128], "float32"),
    "c2": ("sbuf", [128, 128], "float32"),
    "dc": ("sbuf", [128, 128], "float32"),
    "al": ("sbuf", [128, 128], "float32"),
    "tn": ("sbuf", [128, 128], "float32"),
    "den": ("sbuf", [128, 128], "float32"),
    "rd": ("sbuf", [128, 128], "float32"),
    "num": ("sbuf", [128, 128], "float32"),
    "ot": ("sbuf", [128, 128], "float32"),
    "pss": ("psum", [128, 2048], "float32"),
    "pst": ("psum", [128, 1024], "float32"),
    "psa": ("psum", [128, 512], "float32"),
    "psl": ("psum", [128, 512], "float32"),
}
for _i in range(NB):
    SCRATCH["bc%d" % _i] = ("sbuf", [128, W], "float8_e4m3fn_x4")
    SCRATCH["bs%d" % _i] = ("sbuf", [128, W], "uint8")
    SCRATCH["t%d" % _i] = ("sbuf", [128, 512], "float32")
    SCRATCH["pt%d" % _i] = ("sbuf", [128, 512], "bfloat16")
    SCRATCH["pc%d" % _i] = ("sbuf", [128, 128], "float8_e4m3fn_x4")
    SCRATCH["pp%d" % _i] = ("sbuf", [128, 128], "uint8")

SEMAPHORES = (["la", "lb", "lp", "ls", "lq", "st", "rinp", "rinc", "sent", "a10", "a11", "a20", "a21",
               "k1", "k2", "v1", "v2", "pl1", "pl2", "one"] + ["e%d" % _k for _k in range(NEV)])


def _split(mask, k):
    eng = [e for e in range(16) if (mask >> e) & 1]
    n = 1
    while 2 * n * k <= len(eng):
        n *= 2
    return [sum(1 << e for e in eng[i * n:(i + 1) * n]) for i in range(k)], n


def _one_cols(k, n):
    return (128 * k // n) // 4 * 4, (128 * (k + 1) // n) // 4 * 4


def _one_mask(topo, helper, rank_core, dest):
    return topo.mask(helper, rank_core) & topo.mask(helper, dest)


def _plan(T, topo):
    cores = [int(c) for c in T.cores]
    n = len(cores)
    jobs, groups = {}, []
    for j, cj in enumerate(cores):
        dests = [(cores[(j + i) % n], i) for i in range(1, NB)]
        mates = [c for c in range(NSIM) if topo.chip(c) == topo.chip(cj) and c != cj and T.rank_of(c) is None]
        feeds = []
        for h in (0, 1):
            pool = [cj] if h == 0 else []
            pool += [c for c in mates if (topo.die(c) == topo.die(cj)) == (h == 0)]
            pool = [c for c in pool if all(topo.may_write(c, d[0]) for d in dests)]
            for i in range(2):
                groups.append((pool[i], 2 * h + i, dests))
                if pool[i] != cj:
                    feeds.append((pool[i], 2 * h + i))
        for r, q in feeds:
            jobs[r] = ("relay", cj, len([1 for _, x in feeds if PLANE[x][0] == PLANE[q][0]]),
                       len([1 for _, x in feeds if x // 2 == q // 2]))
        jobs[cj] = ("rank", feeds)
    return jobs, groups


def rank_program(g, core, T, topo):
    jobs, groups = _plan(T, topo)
    job = jobs.get(core)
    if job is None:
        return
    u8 = dt.uint8
    sent = [0]
    mine = [gr for gr in groups if gr[0] == core]

    def send(targets, codes, mask=None):
        if not targets:
            return
        masks, n = _split(topo.mask(core, targets[0][0]) if mask is None else mask, len(targets))
        trs = []
        for (dst, out, sem, src), m in zip(targets, masks):
            rid, pid, _ = topo.addr(dst)
            trs.append(RemoteDMATransfer(dst_ids=[DstId(rid=rid, pnc=pid)], dma_engine_mask=m, remote_sem=sem,
                                         src=src.bitcast(u8) if codes else src,
                                         dst=out.bitcast(u8) if codes else out))
            sent[0] += n
        g.remote_dma_fused(trs, local_sem=T.sem.sent)

    def plane_out():
        for _, q, dests in mine:
            w, i = PLANE[q]
            d, k = dests[i]
            send([(d, T["d%s%d" % (w, k)][:], T.sem["%s%d" % (w, k)], T["d" + w][:])], False)

    def codes_out(src):
        for _, q, dests in mine:
            a, b = QUART[q]
            for d, k in dests:
                send([(d, T["bc%d" % k][:, a:b], T.sem["a%d%d" % (k, q // 2)], src)], True)

    if job[0] == "relay":
        hs = [r for r, _ in jobs[job[1]][1]]
        a, b = _one_cols(hs.index(core), len(hs))
        g.vector.memset(T.onet[:], 1.0).then_inc(T.sem.e0, 1)
        g.vector.wait_ge(T.sem.e0, 1)
        g.vector.quantize_mx(T.onec[:], T.ones[:], T.onet[:]).then_inc(T.sem.e1, 1)
        g.wait_ge(T.sem.e1, 1)
        m = _one_mask(topo, core, job[1], mine[0][2][0][0])
        send([(job[1], T.onec[:, a:b], T.sem.one, T.onec[:, a:b])], True, m)
        send([(job[1], T.ones[:, a:b], T.sem.one, T.ones[:, a:b])], False, m)
        g.wait_ge(T.sem.rinp, _split(topo.mask(job[1], core), job[2])[1])
        plane_out()
        g.wait_ge(T.sem.rinc, _split(topo.mask(job[1], core), job[3])[1])
        codes_out(T.rc[:])
        g.wait_ge(T.sem.sent, sent[0])
        return

    feeds = job[1]
    V, S, P, Y = g.vector, g.scalar, g.tensor, g.sync
    AF, OP = ActivationFunctionType, AluOpType
    nev = [0]

    def ev():
        s = T.sem["e%d" % nev[0]]
        nev[0] += 1
        return s

    arrive, plane_in = {}, {}
    for snd, q, dests in groups:
        for i, (d, k) in enumerate(dests):
            if d == core:
                n = _split(topo.mask(snd, d), 1)[1]
                arrive[(k, q // 2)] = arrive.get((k, q // 2), 0) + n
                if PLANE[q][1] == i:
                    plane_in[(PLANE[q][0], k)] = n
    one_in = 0
    for snd, q, dests in groups:
        if (snd, q) in feeds:
            one_in += 2 * _split(_one_mask(topo, snd, core, dests[0][0]), 1)[1]

    LA, LB, LP, LS, LQ = T.sem.la, T.sem.lb, T.sem.lp, T.sem.ls, T.sem.lq
    S.dma_start(T.dk[:], T.ks[:]).then_inc(LP, 16)
    Y.dma_start(T.dv[:], T.vs[:]).then_inc(LP, 16)
    Y.dma_start(T.bc0[:, 384:640].bitcast(u8), T.kc[:, 1024:2048]).then_inc(LB, 16)
    S.dma_start(T.bc0[:, 256:384].bitcast(u8), T.vc[:]).then_inc(LB, 16)
    Y.dma_start(T.bc0[:, 0:256].bitcast(u8), T.kc[:, 0:1024]).then_inc(LA, 16)
    S.dma_start(T.qt[:], T.q[:]).then_inc(LQ, 16)
    S.dma_start(T.bs0[:, 0:512], T.ks[:]).then_inc(LS, 16)
    Y.dma_start(T.bs0[:, 512:640], T.vs[:]).then_inc(LS, 16)

    def cols(t, q):
        return t[:, QUART[q][0]:QUART[q][1]]

    g.wait_ge(LP, 32)
    for w in ("k", "v"):
        send([(r, T["d" + w][:], T.sem.rinp, T["d" + w][:]) for r, q in feeds if PLANE[q][0] == w], False)
    plane_out()
    g.wait_ge(LB, 32)
    send([(r, T.rc[:], T.sem.rinc, cols(T.bc0, q)) for r, q in feeds if q // 2 == 1], True)
    g.wait_ge(LA, 16)
    send([(r, T.rc[:], T.sem.rinc, cols(T.bc0, q)) for r, q in feeds if q // 2 == 0], True)
    for _, q, _ in mine:
        codes_out(cols(T.bc0, q))
    g.wait_ge(T.sem.sent, sent[0])

    e_zero, e_w2, e_q = ev(), ev(), ev()
    V.memset(T.zero[:], 0.0).then_inc(e_zero, 1)
    V.memset(T.wone[0:1, :], 1.0).then_inc(e_w2, 1)
    V.wait_ge(LQ, 16)
    V.quantize_mx(T.qc[:], T.qs[:], T.qt[:]).then_inc(e_q, 1)

    stores = [0]

    def store(out, in_):
        Y.dma_start(out, in_).then_inc(T.sem.st, 16)
        stores[0] += 16

    Y.wait_ge(e_w2, 1)
    store(T.w[1:2, :], T.wone[0:1, :])
    store(T.w[2:3, :], T.wone[0:1, :])

    for k in range(1, NB):
        bs, pl = T["bs%d" % k], T.sem["pl%d" % k]
        Y.wait_ge(T.sem["k%d" % k], plane_in[("k", k)])
        Y.dma_start(bs[:, 0:256], T["dk%d" % k][:, 0:256]).then_inc(pl, 16)
        Y.dma_start(bs[:, 384:640], T["dk%d" % k][:, 256:512]).then_inc(pl, 16)
        Y.wait_ge(T.sem["v%d" % k], plane_in[("v", k)])
        Y.dma_start(bs[:, 256:384], T["dv%d" % k][:]).then_inc(pl, 16)

    e_st = [[ev(), ev()] for _ in range(NB)]
    e_s = [[ev() for _ in range(4)] for _ in range(NB)]
    e_t = [[ev() for _ in range(4)] for _ in range(NB)]
    e_r = [[ev(), ev()] for _ in range(NB)]

    P.wait_ge(e_q, 1)
    P.wait_ge(LS, 32)

    def scores(i):
        bc, bs = T["bc%d" % i], T["bs%d" % i]
        if i > 0:
            P.wait_ge(T.sem["pl%d" % i], 48)
        for h in range(2):
            if i == 0:
                P.wait_ge(LA if h == 0 else LB, 16 if h == 0 else 32)
            else:
                P.wait_ge(T.sem["a%d%d" % (i, h)], arrive[(i, h)])
                P.wait_ge(e_r[i - 1][h], 1)
            k, kp = STCOL[h], (256 * h if i == 0 else STCOL[h])
            P.matmul_mx(T.pst[:, 512 * h:512 * h + 256], T.qc[:], T.qs[:], bc[:, k:k + 256], bs[:, kp:kp + 256],
                        True, True).then_inc(e_st[i][h], 1)
        for b in range(4):
            if i > 0:
                P.wait_ge(e_t[i - 1][b], 1)
            k, kp = KCOL[b], (128 * b if i == 0 else KCOL[b])
            P.matmul_mx(T.pss[:, 512 * b:512 * b + 128], bc[:, k:k + 128], bs[:, kp:kp + 128], T.qc[:], T.qs[:],
                        True, True).then_inc(e_s[i][b], 1)

    def products(i, e_in, ol, oa, start, stop):
        pc, pp = T["pc%d" % i], T["pp%d" % i]
        vp = 512 if i == 0 else VCOL
        P.wait_ge(e_in, 1)
        ml = P.matmul_mx(ol, pc[:], pp[:], T.onec[:], T.ones[:], start, stop)
        ma = P.matmul_mx(oa, T["bc%d" % i][:, VCOL:VCOL + 128], T["bs%d" % i][:, vp:vp + 128], pc[:], pp[:],
                         start, stop)
        return ml, ma

    def scale_and_max(i):
        t = T["t%d" % i]
        for h in range(2):
            V.wait_ge(e_st[i][h], 1)
            V.tensor_reduce(T.red[:, 2 * i + h:2 * i + h + 1], T.pst[:, 512 * h:512 * h + 256], AxisListType.X,
                            OP.max).then_inc(e_r[i][h], 1)
        for b in range(4):
            S.wait_ge(e_s[i][b], 1)
            S.activation(t[:, b:512:4], T.pss[:, 512 * b:512 * b + 128], AF.Identity,
                         scale=SCALE).then_inc(e_t[i][b], 1)

    def spread(z, c, e_z):
        e_x, e1, e2 = ev(), ev(), ev()
        V.wait_ge(e_z, 1)
        V.transpose(c[:], z[:]).then_inc(e_x, 1)
        V.wait_ge(e_x, 1)
        S.wait_ge(e_x, 1)
        V.tensor_copy(c[0:32, 32:64], c[32:64, 32:64]).then_inc(e1, 1)
        V.tensor_copy(c[32:64, 0:32], c[0:32, 0:32]).then_inc(e1, 1)
        S.activation(c[64:96, 96:128], c[96:128, 96:128], AF.Copy).then_inc(e1, 1)
        S.activation(c[96:128, 64:96], c[64:96, 64:96], AF.Copy).then_inc(e1, 1)
        V.wait_ge(e1, 4)
        S.wait_ge(e1, 4)
        V.tensor_copy(c[0:64, 64:128], c[64:128, 64:128]).then_inc(e2, 1)
        S.activation(c[64:128, 0:64], c[0:64, 0:64], AF.Copy).then_inc(e2, 1)
        return e2

    scores(0)
    scale_and_max(0)
    e_m, e_zr, e_z = ev(), ev(), ev()
    V.wait_ge(e_r[0][0], 1)
    V.wait_ge(e_r[0][1], 1)
    V.tensor_reduce(T.mc[:, 0:1], T.red[:, 0:2], AxisListType.X, OP.max).then_inc(e_m, 1)
    V.wait_ge(e_m, 1)
    V.wait_ge(e_zero, 1)
    V.tensor_scalar(T.z01[:], T.zero[:], T.mc[:, 0:1], SCALE, OP.add, OP.mult).then_inc(e_z, 1)
    V.tensor_scalar(T.z0r[:], T.zero[:], T.mc[:, 0:1], None, OP.add).then_inc(e_zr, 1)
    e_c01 = spread(T.z01, T.c01, e_z)
    Y.wait_ge(e_c01, 2)
    store(T.c[0:1, :], T.c01[0:1, :])
    V.wait_ge(e_c01, 2)
    e_sub0, e_exp0, e_p0, e_pq0 = ev(), ev(), ev(), ev()
    for b in range(4):
        V.wait_ge(e_t[0][b], 1)
        V.tensor_tensor(T.t0[:, b:512:4], T.t0[:, b:512:4], T.c01[:], OP.subtract).then_inc(e_sub0, 1)
    S.wait_ge(e_sub0, 4)
    S.activation(T.pt0[:], T.t0[:], AF.Exp).then_inc(e_exp0, 1)
    V.wait_ge(e_exp0, 1)
    V.tensor_scalar(T.pt0[:], T.pt0[:], FLOOR, None, OP.max).then_inc(e_p0, 1)
    V.wait_ge(e_p0, 1)
    V.quantize_mx(T.pc0[:], T.pp0[:], T.pt0[:]).then_inc(e_pq0, 1)
    Y.wait_ge(e_p0, 1)
    store(T.p[0], T.pt0[:])
    e_l01, e_a01 = ev(), ev()

    scores(1)
    scores(2)
    P.wait_ge(T.sem.one, one_in)
    ml, ma = products(0, e_pq0, T.psl[:, 0:128], T.psa[:, 0:128], True, True)
    ml.then_inc(e_l01, 1)
    ma.then_inc(e_a01, 1)
    scale_and_max(1)
    e_z1, e_za, e_z2 = ev(), ev(), ev()
    V.wait_ge(e_r[1][0], 1)
    V.wait_ge(e_r[1][1], 1)
    V.wait_ge(e_zr, 1)
    V.tensor_scalar(T.z1r[:], T.z0r[:], T.red[:, 2:3], T.red[:, 3:4], OP.max, OP.max).then_inc(e_z1, 1)
    scale_and_max(2)
    V.wait_ge(e_z1, 1)
    V.wait_ge(e_r[2][0], 1)
    V.tensor_scalar(T.z2a[:], T.z1r[:], T.red[:, 4:5], None, OP.max).then_inc(e_za, 1)
    V.wait_ge(e_za, 1)
    V.wait_ge(e_r[2][1], 1)
    V.tensor_scalar(T.z2[:], T.z2a[:], T.red[:, 5:6], SCALE, OP.max, OP.mult).then_inc(e_z2, 1)
    e_c2 = spread(T.z2, T.c2, e_z2)
    Y.wait_ge(e_c2, 2)
    store(T.c[1:2, :], T.c2[0:1, :])
    store(T.c[2:3, :], T.c2[0:1, :])
    V.wait_ge(e_c2, 2)
    e_sb = [[ev() for _ in range(4)] for _ in range(2)]
    e_ex1, e_ex = ev(), [ev() for _ in range(4)]
    e_p1, e_pq1, e_p2, e_pq2 = ev(), ev(), ev(), ev()

    def shift_exp(i, b):
        t, pt = T["t%d" % i], T["pt%d" % i]
        V.wait_ge(e_t[i][b], 1)
        V.tensor_tensor(t[:, b:512:4], t[:, b:512:4], T.c2[:], OP.subtract).then_inc(e_sb[i - 1][b], 1)
        S.wait_ge(e_sb[i - 1][b], 1)
        S.activation(pt[:, b:512:4], t[:, b:512:4], AF.Exp).then_inc(e_ex1 if i == 1 else e_ex[b], 1)

    for b in range(4):
        shift_exp(1, b)
    shift_exp(2, 0)
    shift_exp(2, 1)
    V.wait_ge(e_ex1, 4)
    V.tensor_scalar(T.pt1[:], T.pt1[:], FLOOR, None, OP.max).then_inc(e_p1, 1)
    V.wait_ge(e_p1, 1)
    V.quantize_mx(T.pc1[:], T.pp1[:], T.pt1[:]).then_inc(e_pq1, 1)
    Y.wait_ge(e_p1, 1)
    store(T.p[1], T.pt1[:])
    shift_exp(2, 2)
    shift_exp(2, 3)
    for b in range(4):
        V.wait_ge(e_ex[b], 1)
        V.tensor_scalar(T.pt2[:, b:512:4], T.pt2[:, b:512:4], FLOOR, None, OP.max).then_inc(e_p2, 1)
    V.wait_ge(e_p2, 4)
    V.quantize_mx(T.pc2[:], T.pp2[:], T.pt2[:]).then_inc(e_pq2, 1)
    Y.wait_ge(e_p2, 4)
    store(T.p[2], T.pt2[:])
    e_l2, e_a2 = ev(), ev()
    products(1, e_pq1, T.pst[:, 0:128], T.pst[:, 512:640], True, False)
    ml, ma = products(2, e_pq2, T.pst[:, 0:128], T.pst[:, 512:640], False, True)
    ml.then_inc(e_l2, 1)
    ma.then_inc(e_a2, 1)

    e_dk, e_ak, e_dc, e_al, e_tn, e_den, e_rd, e_zq, e_num, e_o = [ev() for _ in range(10)]
    V.tensor_tensor(T.mc[:, 3:4], T.z01[:, 0:1], T.z2[:, 0:1], OP.subtract).then_inc(e_dk, 1)
    V.tensor_tensor(T.dc[:], T.c01[:], T.c2[:], OP.subtract).then_inc(e_dc, 1)
    S.wait_ge(e_dk, 1)
    S.activation(T.md[:, 0:1], T.mc[:, 3:4], AF.Exp).then_inc(e_ak, 1)
    S.wait_ge(e_dc, 1)
    S.activation(T.al[:], T.dc[:], AF.Exp).then_inc(e_al, 1)
    Y.wait_ge(e_al, 1)
    store(T.w[0:1, :], T.al[0:1, :])
    V.wait_ge(e_ak, 1)
    V.wait_ge(e_l01, 1)
    V.wait_ge(e_l2, 1)
    V.tensor_scalar(T.md[:, 1:2], T.psl[:, 0:1], T.md[:, 0:1], T.pst[:, 0:1], OP.mult, OP.add).then_inc(e_den, 1)
    V.wait_ge(e_den, 1)
    V.reciprocal(T.md[:, 2:3], T.md[:, 1:2]).then_inc(e_rd, 1)
    V.wait_ge(e_rd, 1)
    V.tensor_scalar(T.den[:], T.zero[:], T.md[:, 2:3], None, OP.add).then_inc(e_zq, 1)
    V.wait_ge(e_al, 1)
    V.wait_ge(e_a01, 1)
    V.tensor_tensor(T.tn[:], T.psa[:, 0:128], T.al[:], OP.mult).then_inc(e_tn, 1)
    e_r2 = spread(T.den, T.rd, e_zq)
    V.wait_ge(e_tn, 1)
    V.wait_ge(e_a2, 1)
    V.tensor_tensor(T.num[:], T.pst[:, 512:640], T.tn[:], OP.add).then_inc(e_num, 1)
    V.wait_ge(e_r2, 2)
    V.wait_ge(e_num, 1)
    V.tensor_tensor(T.ot[:], T.num[:], T.rd[:], OP.mult).then_inc(e_o, 1)
    Y.wait_ge(e_o, 1)
    store(T.o[:], T.ot[:])
    Y.wait_ge(T.sem.st, stores[0])
